import numpy as np
import ml_dtypes


def mxq(x, axis, fmt="e4m3"):
    dtype, down = {"e4m3": (ml_dtypes.float8_e4m3fn, 7), "e5m2": (ml_dtypes.float8_e5m2, 14)}[fmt]
    v = np.moveaxis(np.asarray(x, np.float32).astype(ml_dtypes.bfloat16).astype(np.float64), axis, -1)
    blocks = v.reshape(v.shape[:-1] + (-1, 32))
    amax = np.abs(blocks).max(-1, keepdims=True)
    byte = np.maximum(np.where(amax > 0, np.frexp(amax)[1] - 1 + 127, 0) - down, 1)
    scale = np.exp2(byte - 127.0)
    codes = (blocks / scale).astype(np.float32).astype(dtype).astype(np.float64)
    return np.moveaxis((codes * scale).reshape(v.shape), -1, axis)


WIDE = False


def mx_kscale(k):
    if not WIDE:
        return np.ones(k)
    levels = np.array([10, -10, 5, -5, 0])
    if k % 512:
        return np.exp2(np.random.permutation(np.resize(levels, k // 32))).repeat(32)
    a = np.empty((k // 512, 16))
    for p in range(k // 512):
        a[p, :8] = np.random.permutation(np.resize(levels, 8))
        for g in range(8):
            far = levels[np.abs(levels - a[p, g]) >= 10]
            a[p, g + 8] = far[np.random.randint(len(far))]
    return np.exp2(a.ravel()).repeat(32)


def f64(x):
    return np.asarray(x).astype(np.float64)


def striped(idx):
    return np.tile(np.asarray(idx).reshape(-1, 16).T, (8, 1)).astype(np.uint16)


def unstriped(offs):
    return offs[:16].T.reshape(-1).astype(np.int64)


E2M1 = np.array([0.0, 0.5, 1.0, 1.5, 2.0, 3.0, 4.0, 6.0, -0.0, -0.5, -1.0, -1.5, -2.0, -3.0, -4.0, -6.0])


def pack_weight(w, fmt):
    k, n = w.shape
    w = f64(np.asarray(w, np.float32).astype(ml_dtypes.bfloat16)).reshape(k // 32, 32, n)
    amax = np.abs(w).max(1)
    if fmt == "e4m3":
        byte = np.frexp(amax)[1] - 1 + 127 - 7
    else:
        mant, ex = np.frexp(amax / 6.0)
        byte = np.where(mant > 0.5, ex, ex - 1) + 127
    byte = np.clip(np.where(amax > 0, byte, 1), 1, 254)
    scaled = (w * np.exp2(127.0 - byte)[:, None, :]).reshape(k, n).astype(np.float32)
    by_word = np.ascontiguousarray(scaled.reshape(k // 512, 128, 4, n).transpose(0, 1, 3, 2))
    if fmt == "e4m3":
        words = by_word.astype(ml_dtypes.float8_e4m3fn).view(np.uint8)
    else:
        c = by_word.astype(ml_dtypes.float4_e2m1fn).view(np.uint8) & 0xF
        words = (c[..., 0::2] | (c[..., 1::2] << 4)).reshape(k // 512, 128, 2 * n)
    return np.ascontiguousarray(words), np.ascontiguousarray(byte.astype(np.uint8).reshape(k // 512, 16, n))


def unpack_weight(words, scales, fmt):
    g, _, n = scales.shape
    words = np.ascontiguousarray(words).reshape(g, 128, n, -1)
    if fmt == "e4m3":
        vals = words.view(ml_dtypes.float8_e4m3fn).astype(np.float64)
    else:
        nib = np.empty((g, 128, n, 4), np.uint8)
        nib[..., 0::2] = words & 0xF
        nib[..., 1::2] = words >> 4
        vals = E2M1[nib]
    vals = vals * np.repeat(np.exp2(scales.astype(np.float64) - 127.0), 8, axis=1)[..., None]
    return vals.transpose(0, 1, 3, 2).reshape(g * 512, n)


def bf(x):
    return np.asarray(x, np.float32).astype(ml_dtypes.bfloat16)


def planes(Y):
    r, m = Y.shape
    b = f64(bf(Y)).reshape(r // 32, 32, m)
    amax = np.abs(b).max(1)
    byte = np.clip(np.where(amax > 0, np.frexp(amax)[1] - 1 + 127 - 7, 1), 1, 254)
    codes = (b * np.exp2(127.0 - byte)[:, None, :]).reshape(r, m).astype(np.float32).astype(ml_dtypes.float8_e4m3fn).view(np.uint8)
    words = codes.reshape(r // 512, 128, 4, m).transpose(0, 1, 3, 2)
    return np.ascontiguousarray(words), np.ascontiguousarray(byte.astype(np.uint8).reshape(r // 512, 16, m))


K, R, F, T, J, G = 512, 512, 512, 2048, 512, 64


def setup_inputs():
    n = np.random.standard_normal
    idx = np.random.permutation(T)[:J]
    fk = mx_kscale(K)
    fr = mx_kscale(R)
    dtabp = pack_weight(n((K, T)) / fk[:, None], "e4m3")
    tabp = pack_weight(n((K, T)) / fk[:, None], "e4m3")
    return {
        "dtab_words": dtabp[0],
        "dtab_scales": dtabp[1],
        "tab_words": tabp[0],
        "tab_scales": tabp[1],
        "w1": (n((K, R)) * 1 / np.sqrt(K) * fk[:, None]).astype(np.float32),
        "share": (np.random.uniform(0.3, 1.2, (R, 1))).astype(np.float32),
        "rs": (np.random.uniform(0.5, 2.0, (R, 1)) * fr[:, None]).astype(np.float32),
        "wor": (n((R, F)) * 1 / np.sqrt(R) / fr[:, None]).astype(np.float32),
        "res": (n((F, G)) * 0.5).astype(np.float32),
        "offs": striped(idx),
    }


def reference(dtab_words, dtab_scales, tab_words, tab_scales, w1, share, rs, wor, res, offs):
    idx = unstriped(offs)
    dtabu = unpack_weight(dtab_words, dtab_scales, "e4m3")
    tabu = unpack_weight(tab_words, tab_scales, "e4m3")
    w1q = mxq(f64(w1), 0, "e4m3")
    tabidxg = tabu[:, idx]
    a = w1q.T @ tabidxg
    dtabidxg = dtabu[:, idx]
    ta = w1q.T @ dtabidxg
    m1 = a.reshape(R, G, J // G).mean(axis=2)
    v1 = np.sqrt(np.square(a).reshape(R, G, J // G).mean(axis=2) - np.square(m1) + 0.05)
    u1 = np.tanh(v1 + m1 * f64(share))
    tm1 = ta.reshape(R, G, J // G).mean(axis=2)
    tv1 = ((ta * a * 2.0).reshape(R, G, J // G).mean(axis=2) - tm1 * m1 * 2.0) * 0.5 / v1
    tu1 = (tv1 + tm1 * f64(share)) * (1.0 - np.square(u1))
    fo1 = tu1 * f64(rs)
    worq = mxq(f64(wor), 0, "e4m3")
    fo1q = mxq(fo1, 0, "e4m3")
    yo = worq.T @ fo1q
    y = yo + f64(res)
    words, scales = planes(y)
    return y, words, scales

from contextlib import ExitStack

import concourse.mybir as mybir
from concourse.masks import make_identity

K, R, F, T, J, G = 512, 512, 512, 2048, 512, 64
P = 128
PACK = 4
GROUP = J // G
EPS = 0.05
FLOPS = 2 * 2 * K * R * J + 2 * R * F * G

F32 = mybir.dt.float32
BF16 = mybir.dt.bfloat16
I32 = mybir.dt.int32
U32 = mybir.dt.uint32
U16 = mybir.dt.uint16
U8 = mybir.dt.uint8
FP8X4 = mybir.dt.float8_e4m3fn_x4
ALU = mybir.AluOpType
ACT = mybir.ActivationFunctionType


def tile_attend_tspreadpool_o_pl_kernel(
    tc, dtab_words, dtab_scales, tab_words, tab_scales, w1, share, rs, wor, res, offs, out_0, out_1, out_2
):
    nc = tc.nc
    with ExitStack() as ctx:
        sb = ctx.enter_context(tc.tile_pool(name="sb", bufs=1))
        ps = ctx.enter_context(tc.psum_pool(name="ps", bufs=1))

        def bank(n, name, shape):
            return ps.tile(shape, F32, name=name, tag="bank%d" % n)

        offsets = sb.tile([P, J // 16], U16, name="offsets")
        nc.sync.dma_start(offsets[:], offs)

        def load_scale_rows(queue, zeroing, scales, name):
            window = sb.tile([P, T], U8, name=name, align_bytes=64)
            if zeroing is None:
                for q in range(4):
                    queue.dma_start(
                        out=window[32 * q : 32 * q + 32, :].bitcast(I32),
                        in_=scales[0, 4 * q : 4 * q + 4, :].bitcast(I32).unsqueeze(0).to_broadcast([8, 4, T // 4]),
                    )
                return window
            zeroing.memset(window[:].bitcast(I32), 0)
            for q in range(4):
                queue.dma_start(
                    out=window[32 * q : 32 * q + 4, :].bitcast(I32),
                    in_=scales[0, 4 * q : 4 * q + 4, :].bitcast(I32),
                )
            return window

        def load_words(words, name):
            window = sb.tile([P, T], U32, name=name, align_bytes=64)
            nc.sync.dma_start(
                out=window[:].bitcast(I32), in_=words[0].rearrange("p n t -> p (n t)").bitcast(I32)
            )
            return window

        def load_rows(queue, matrix, name, tag):
            raw = sb.tile([P, PACK, matrix.shape[1]], F32, name=name, tag=tag, align_bytes=64)
            queue.dma_start(out=raw[:], in_=matrix.rearrange("(p j) c -> p j c", j=PACK))
            return raw

        share_sb = load_rows(nc.scalar, share, "share_sb", "column")
        ident = sb.tile([P, P], F32, name="ident", align_bytes=64)
        make_identity(nc, ident[:])
        tab_scale_win = load_scale_rows(nc.sync, None, tab_scales, "tab_scale_win")
        dtab_scale_win = load_scale_rows(nc.scalar, nc.vector, dtab_scales, "dtab_scale_win")
        w1_raw = load_rows(nc.sync, w1, "w1_raw", "weights")
        tab_word_win = load_words(tab_words, "tab_word_win")
        dtab_word_win = load_words(dtab_words, "dtab_word_win")

        def gather_scales(window, name):
            got = sb.tile([P, J], U8, name=name, align_bytes=64)
            nc.vector.tensor_copy(got[:], window[:].indirect(offsets[:]))
            return got

        def deal(raw, name, split):
            grouped = sb.tile([P, PACK, P, PACK], BF16, name=name, align_bytes=64)
            dst = grouped[:].rearrange("p t m j -> p m j t")
            src = raw[:].rearrange("p j (m t) -> p m j t", t=PACK)
            nc.vector.tensor_copy(out=dst[:, 0:split], in_=src[:, 0:split])
            if split < P:
                nc.scalar.copy(out=dst[:, split:P], in_=src[:, split:P])
            return grouped

        def quantise(grouped_flat, width, name):
            codes = sb.tile([P, width], U32, name=name + "_codes", align_bytes=64)
            plane = sb.tile([P, width], U8, name=name + "_plane", align_bytes=64)
            nc.vector.quantize_mx(out=codes[:].bitcast(FP8X4), scales=plane[:], in_=grouped_flat)
            return codes, plane

        tab_scale = gather_scales(tab_scale_win, "tab_scale")
        w1_grouped = deal(w1_raw, "w1_grouped", 80)
        wor_raw = load_rows(nc.sync, wor, "wor_raw", "weights")
        w1_codes, w1_plane = quantise(w1_grouped[:].rearrange("p t m j -> p (t m j)"), R, "w1")

        share_b = sb.tile([P, PACK, G], F32, name="share_b", tag="quarter", align_bytes=64)
        nc.scalar.activation(share_b[:], share_sb[:].to_broadcast([P, PACK, G]), ACT.Copy)
        share_ps = bank(7, "share_ps", [P, 2, P])
        for u in range(2):
            nc.tensor.transpose(
                share_ps[:, u, :], share_b[:, 2 * u : 2 * u + 2, :].rearrange("p t g -> p (t g)"), ident[:]
            )
        share_t = sb.tile([P, 2 * P], F32, name="share_t", align_bytes=64)
        nc.scalar.copy(out=share_t[:], in_=share_ps[:].rearrange("p u c -> p (u c)"))
        rs_sb = load_rows(nc.sync, rs, "rs_sb", "column")
        res_sb = load_rows(nc.sync, res, "res_sb", "quarter")

        HALF = J // 2

        def first_layer(word_win, scale, first_bank, name):
            words = sb.tile([P, J], U32, name=name + "_words", align_bytes=64)
            banks = [bank(first_bank + t, "%s_ps%d" % (name, t), [P, J]) for t in range(PACK)]
            for h in range(2):
                cols = slice(h * HALF, (h + 1) * HALF)
                nc.vector.tensor_copy(
                    words[:, cols], word_win[:].indirect(offsets[:, h * HALF // 16 : (h + 1) * HALF // 16])
                )
                for t in range(PACK):
                    rows = slice(t * P, (t + 1) * P)
                    nc.tensor.matmul_mx(
                        out=banks[t][:, cols],
                        lhsT=w1_codes[:, rows].bitcast(FP8X4),
                        lhsT_scale=w1_plane[:, rows],
                        rhs=words[:, cols].bitcast(FP8X4),
                        rhs_scale=scale[:, cols],
                        start=True,
                        stop=True,
                    )
            return banks

        def pair_tiles(name):
            return [sb.tile([P, GROUP, 2, G], F32, name="%s%d" % (name, u), align_bytes=64) for u in range(2)]

        def place(tiles, t):
            return tiles[t // 2][:, :, t % 2, :]

        def by_member(b):
            return b[:].rearrange("p (g i) -> p i g", i=GROUP)

        def group_sums(tiles, out_bank, u):
            for i in range(GROUP):
                nc.tensor.matmul(
                    out_bank[:, u * P : (u + 1) * P],
                    tiles[u][:, i].rearrange("p t g -> p (t g)"),
                    ident[:],
                    is_transpose=True,
                    start=(i == 0),
                    stop=(i == GROUP - 1),
                )

        a_ps = first_layer(tab_word_win, tab_scale, 0, "a")
        a_sb, sq_sb, ta_sb, prod_sb = pair_tiles("a_sb"), pair_tiles("sq_sb"), pair_tiles("ta_sb"), pair_tiles("prod_sb")
        dtab_scale = gather_scales(dtab_scale_win, "dtab_scale")
        ta_ps = first_layer(dtab_word_win, dtab_scale, 4, "ta")
        for t in range(PACK):
            nc.scalar.activation(place(sq_sb, t), by_member(a_ps[t]), ACT.Square)
            if t < 2:
                nc.scalar.copy(out=place(a_sb, t), in_=by_member(a_ps[t]))
            else:
                nc.vector.tensor_copy(out=place(a_sb, t), in_=by_member(a_ps[t]))
        sum_a = bank(0, "sum_a", [P, 2 * P])
        sum_sq = bank(1, "sum_sq", [P, 2 * P])
        for u in range(2):
            group_sums(a_sb, sum_a, u)
            group_sums(sq_sb, sum_sq, u)

        def small(name):
            return sb.tile([P, 2 * P], F32, name=name, align_bytes=64)

        inv = 1.0 / GROUP
        mean_sq, spread, rinv, root, mean_share = (
            small("mean_sq"), small("spread"), small("rinv"), small("root"), small("mean_share")
        )
        nc.scalar.activation(mean_sq[:], sum_a[:], ACT.Square, scale=inv)
        nc.vector.scalar_tensor_tensor(spread[:], sum_sq[:], inv, mean_sq[:], ALU.mult, ALU.subtract)
        nc.scalar.activation(rinv[:], spread[:], ACT.Abs_reciprocal_sqrt, bias=EPS)
        nc.vector.scalar_tensor_tensor(mean_share[:], sum_a[:], inv, share_t[:], ALU.mult, ALU.mult)
        nc.vector.scalar_tensor_tensor(root[:], spread[:], EPS, rinv[:], ALU.add, ALU.mult)

        def turn_back(out_bank, first, second):
            for u in range(2):
                cols = slice(u * P, (u + 1) * P)
                nc.tensor.matmul(out_bank[:, cols], first[:, cols], ident[:], is_transpose=True, start=True, stop=False)
                nc.tensor.matmul(out_bank[:, cols], second[:, cols], ident[:], is_transpose=True, start=False, stop=True)

        def g_major(b):
            return b[:].rearrange("p (t g) -> p g t", g=G)

        for t in range(PACK):
            nc.scalar.copy(out=place(ta_sb, t), in_=by_member(ta_ps[t]))
        for t in range(2):
            nc.vector.tensor_tensor(place(prod_sb, t), by_member(ta_ps[t]), place(a_sb, t), ALU.mult)
        for members in (slice(0, GROUP // 2), slice(GROUP // 2, GROUP)):
            for t in range(2, PACK):
                nc.vector.tensor_tensor(
                    place(prod_sb, t)[:, members], by_member(ta_ps[t])[:, members], place(a_sb, t)[:, members], ALU.mult
                )
        sum_ta = bank(2, "sum_ta", [P, 2 * P])
        sum_prod = bank(3, "sum_prod", [P, 2 * P])
        for u in range(2):
            group_sums(ta_sb, sum_ta, u)
            group_sums(prod_sb, sum_prod, u)

        arg_ps = bank(4, "arg_ps", [P, 2 * P])
        turn_back(arg_ps, mean_share, root)
        tanh = sb.tile([P, G, PACK], F32, name="tanh", align_bytes=64)
        nc.scalar.activation(tanh[:], g_major(arg_ps), ACT.Tanh)
        tanh_sq = sb.tile([P, G, PACK], F32, name="tanh_sq", align_bytes=64)
        nc.scalar.activation(tanh_sq[:], tanh[:], ACT.Square)

        pull, weight, ta_term, prod_term = small("pull"), small("weight"), small("ta_term"), small("prod_term")
        nc.vector.scalar_tensor_tensor(pull[:], sum_a[:], -inv, rinv[:], ALU.mult, ALU.mult)
        nc.vector.tensor_tensor(weight[:], pull[:], share_t[:], ALU.add)
        nc.vector.tensor_tensor(ta_term[:], sum_ta[:], weight[:], ALU.mult)
        nc.vector.tensor_tensor(prod_term[:], sum_prod[:], rinv[:], ALU.mult)
        change_ps = bank(5, "change_ps", [P, 2 * P])
        turn_back(change_ps, ta_term, prod_term)

        wor_grouped = sb.tile([P, PACK, P, PACK], BF16, name="wor_grouped", align_bytes=64)
        nc.gpsimd.tensor_scalar(
            wor_grouped[:].rearrange("p t m j -> p m j t"),
            wor_raw[:].rearrange("p j (m t) -> p m j t", t=PACK),
            1.0, 0.0, ALU.mult, ALU.add,
        )
        wor_codes, wor_plane = quantise(wor_grouped[:].rearrange("p t m j -> p (t m j)"), F, "wor")

        slope = sb.tile([P, G, PACK], F32, name="slope", align_bytes=64)
        rs_b = rs_sb[:].rearrange("p t o -> p o t").to_broadcast([P, G, PACK])
        nc.vector.scalar_tensor_tensor(slope[:], tanh_sq[:], -1.0, rs_b, ALU.add, ALU.mult)
        fo = sb.tile([P, G, PACK], BF16, name="fo", align_bytes=64)
        nc.vector.scalar_tensor_tensor(fo[:], g_major(change_ps), -inv, slope[:], ALU.mult, ALU.mult)
        fo_codes, fo_plane = quantise(fo[:].rearrange("p g t -> p (g t)"), G, "fo")

        yo = bank(6, "yo", [P, PACK, G])
        for j in range(PACK):
            rows = slice(j * P, (j + 1) * P)
            nc.tensor.matmul_mx(
                out=yo[:, j, :],
                lhsT=wor_codes[:, rows].bitcast(FP8X4),
                lhsT_scale=wor_plane[:, rows],
                rhs=fo_codes[:].bitcast(FP8X4),
                rhs_scale=fo_plane[:],
                start=True,
                stop=True,
            )
        y_bf = sb.tile([P, G, PACK], BF16, name="y_bf", align_bytes=64)
        nc.vector.tensor_tensor(
            y_bf[:], yo[:].rearrange("p j g -> p g j"), res_sb[:].rearrange("p j g -> p g j"), ALU.add
        )
        y = sb.tile([P, PACK, G], F32, name="y", align_bytes=64)
        nc.vector.tensor_tensor(y[:], yo[:], res_sb[:], ALU.add)
        y_codes, y_plane = quantise(y_bf[:].rearrange("p g j -> p (g j)"), G, "y")
        nc.sync.dma_start(out=out_0.rearrange("(p j) g -> p j g", j=PACK), in_=y[:])
        nc.scalar.dma_start(
            out=out_1[0].rearrange("p n t -> p (n t)").bitcast(I32), in_=y_codes[:].bitcast(I32)
        )
        for q in range(4):
            queue = nc.sync if q % 2 == 0 else nc.scalar
            queue.dma_start(
                out=out_2[0, 4 * q : 4 * q + 4, :].bitcast(I32),
                in_=y_plane[32 * q : 32 * q + 4, :].bitcast(I32),
            )
